import numpy as np
import ml_dtypes


def mxq(x, axis, fmt="e4m3"):
    dtype, down = {"e4m3": (ml_dtypes.float8_e4m3fn, 7), "e5m2": (ml_dtypes.float8_e5m2, 14)}[fmt]
    v = np.moveaxis(np.asarray(x, np.float32).astype(ml_dtypes.bfloat16).astype(np.float64), axis, -1)
    blocks = v.reshape(v.shape[:-1] + (-1, 32))
    amax = np.abs(blocks).max(-1, keepdims=True)
    byte = np.maximum(np.where(amax > 0, np.frexp(amax)[1] - 1 + 127, 0) - down, 1)
    scale = np.exp2(byte - 127.0)
    codes = (blocks / scale).astype(np.float32).astype(dtype).astype(np.float64)
    return np.moveaxis((codes * scale).reshape(v.shape), -1, axis)


WIDE = False


def mx_kscale(k):
    if not WIDE:
        return np.ones(k)
    levels = np.array([10, -10, 5, -5, 0])
    if k % 512:
        return np.exp2(np.random.permutation(np.resize(levels, k // 32))).repeat(32)
    a = np.empty((k // 512, 16))
    for p in range(k // 512):
        a[p, :8] = np.random.permutation(np.resize(levels, 8))
        for g in range(8):
            far = levels[np.abs(levels - a[p, g]) >= 10]
            a[p, g + 8] = far[np.random.randint(len(far))]
    return np.exp2(a.ravel()).repeat(32)


BF16 = ml_dtypes.bfloat16


def bf(x):
    return np.asarray(x, np.float32).astype(BF16)


def f64(x):
    return np.asarray(x).astype(np.float64)


E2M1 = np.array([0.0, 0.5, 1.0, 1.5, 2.0, 3.0, 4.0, 6.0, -0.0, -0.5, -1.0, -1.5, -2.0, -3.0, -4.0, -6.0])


def pack_weight(w, fmt):
    k, n = w.shape
    w = f64(bf(w)).reshape(k // 32, 32, n)
    amax = np.abs(w).max(1)
    if fmt == "e4m3":
        byte = np.frexp(amax)[1] - 1 + 127 - 7
    else:
        mant, ex = np.frexp(amax / 6.0)
        byte = np.where(mant > 0.5, ex, ex - 1) + 127
    byte = np.clip(np.where(amax > 0, byte, 1), 1, 254)
    scaled = (w * np.exp2(127.0 - byte)[:, None, :]).reshape(k, n).astype(np.float32)
    by_word = np.ascontiguousarray(scaled.reshape(k // 512, 128, 4, n).transpose(0, 1, 3, 2))
    if fmt == "e4m3":
        words = by_word.astype(ml_dtypes.float8_e4m3fn).view(np.uint8)
    else:
        c = by_word.astype(ml_dtypes.float4_e2m1fn).view(np.uint8) & 0xF
        words = c[..., 0::2] | (c[..., 1::2] << 4)
    return np.ascontiguousarray(words), np.ascontiguousarray(byte.astype(np.uint8).reshape(k // 512, 16, n))


def unpack_weight(words, scales, fmt):
    g, p, n, _ = words.shape
    if fmt == "e4m3":
        vals = np.ascontiguousarray(words).view(ml_dtypes.float8_e4m3fn).astype(np.float64)
    else:
        nib = np.empty((g, p, n, 4), np.uint8)
        nib[..., 0::2] = words & 0xF
        nib[..., 1::2] = words >> 4
        vals = E2M1[nib]
    vals = vals * np.repeat(np.exp2(scales.astype(np.float64) - 127.0), 8, axis=1)[..., None]
    return vals.transpose(0, 1, 3, 2).reshape(g * 512, n)
def pack4(w):
    words, scales = pack_weight(w, "e2m1")
    return words.reshape(words.shape[0], 128, -1), scales


def unpack4(words, scales):
    return unpack_weight(words.reshape(words.shape[0], 128, -1, 2), scales, "e2m1")


A, K, U, Z = 2048, 512, 1024, 1024

GAMMA = 1.5
BETA_R = 0.96
DECAY = 5.0


def setup_inputs():
    s, v, t = mx_kscale(K), mx_kscale(U), mx_kscale(Z)
    xa, xk, xu, xz = np.linspace(0, 1, A), np.linspace(0, 1, K), np.linspace(0, 1, U), np.linspace(0, 1, Z)
    basis = np.exp(0.5 * np.random.standard_normal((A, K)) - DECAY * np.abs(xa[:, None] - xk))
    basis = basis / basis.sum(1, keepdims=True)
    theta = np.exp(0.5 * np.random.standard_normal((K, Z))) * (0.3 + 2.0 * xk[:, None]) * (0.5 + xz)
    leave = np.exp(np.random.standard_normal((U, Z)) - DECAY * np.abs(xu[:, None] - xz))
    leave = leave / leave.sum(0, keepdims=True)
    arrive = np.exp(np.random.standard_normal((U, Z)) - DECAY * np.abs(xu[:, None] - xz))
    arrive = arrive / arrive.mean(1, keepdims=True)
    price = BETA_R * np.exp(0.2 * np.random.standard_normal(Z)) / Z
    leave_words, leave_scales = pack4(leave * v[:, None])
    arrive_words, arrive_scales = pack4(arrive / v[:, None] / t)
    return {"basis": bf(basis * s), "theta": bf(theta / s[:, None]), "price": bf(price * t),
            "leave_words": leave_words, "leave_scales": leave_scales,
            "arrive_words": arrive_words, "arrive_scales": arrive_scales}


def reference(basis, theta, price, leave_words, leave_scales, arrive_words, arrive_scales):
    c_next = mxq(f64(basis), 1, "e4m3") @ mxq(f64(theta), 0, "e4m3")
    trans = unpack4(leave_words, leave_scales).T @ unpack4(arrive_words, arrive_scales)
    mu = f64(price) * c_next ** (-GAMMA)
    emu = mxq(mu, 1, "e4m3") @ mxq(trans, 1, "e4m3").T
    return emu ** (-1.0 / GAMMA)

@@ -1,0 +1,378 @@
+from contextlib import ExitStack
+
+import concourse.mybir as mybir
+from concourse.masks import make_identity
+
+A, K, U, Z = 2048, 512, 1024, 1024
+FLOPS = 2 * (A * K * Z + Z * U * Z + A * Z * Z)
+
+F32 = mybir.dt.float32
+BF16 = mybir.dt.bfloat16
+I32 = mybir.dt.int32
+U32 = mybir.dt.uint32
+U8 = mybir.dt.uint8
+FP8X4 = mybir.dt.float8_e4m3fn_x4
+FP4X4 = mybir.dt.float4_e2m1fn_x4
+ACT = mybir.ActivationFunctionType
+ALU = mybir.AluOpType
+
+P = 128
+
+
+def tile_endogenous_grid_euler_step_s12_kernel(
+    tc, basis, theta, price, leave_words, leave_scales, arrive_words, arrive_scales, out
+):
+    nc = tc.nc
+    with ExitStack() as ctx:
+        keep = ctx.enter_context(tc.tile_pool(name="keep", bufs=1))
+        stage = ctx.enter_context(tc.tile_pool(name="stage", bufs=2))
+        psum = ctx.enter_context(tc.psum_pool(name="psum", bufs=4))
+        ctx.enter_context(
+            tc.manual_schedule(
+                engines={mybir.EngineType.Activation, mybir.EngineType.Pool, mybir.EngineType.SP}
+            )
+        )
+
+        def kt(name, shape, dtype):
+            return keep.tile(shape, dtype, name=name, tag=name, align_bytes=64)
+
+        ident = kt("ident", [P, P], F32)
+        one = kt("one", [P, 1], F32)
+        rows = kt("rows", [P, P], BF16)
+        rows32 = kt("rows32", [P, P], F32)
+        price_col = kt("price_col", [P, 8], F32)
+        expo = kt("expo", [P, 8], F32)
+        csc = kt("csc", [P, 8], F32)
+        l_words = kt("l_words", [P, 2, 2048], U8)
+        r_words = kt("r_words", [P, 2, 2048], U8)
+        rp_words = kt("rp_words", [P, 2, 2048], U8)
+        l_plane = kt("l_plane", [P, 2, 1024], U8)
+        r_plane = kt("r_plane", [P, 2, 1024], U8)
+        rp_plane = kt("rp_plane", [P, 2, 1024], U8)
+
+        def as_i32(t):
+            return t[:].rearrange("p g w -> p (g w)").bitcast(I32)
+
+        th_raw = []
+        for h in range(2):
+            t_ = kt("th_raw%d" % h, [P, 4, 512], BF16)
+            th_raw.append(t_)
+        ba_raw = []
+        for c in range(4):
+            b_ = kt("ba_raw%d" % c, [P, 4, 512], BF16)
+            ba_raw.append(b_)
+
+        def load_theta(h):
+            nc.sync.dma_start(
+                out=th_raw[h][:],
+                in_=theta[:, 512 * h : 512 * h + 512].rearrange("(p j) z -> p j z", j=4),
+            )
+
+        def load_basis(c):
+            nc.sync.dma_start(
+                out=ba_raw[c][:],
+                in_=basis[512 * c : 512 * c + 512, :].rearrange("(p r) k -> p r k", r=4),
+            )
+
+        nc.vector.memset(rows[:], 0.0)
+        nc.vector.memset(one[:], 1.0)
+        nc.vector.memset(as_i32(l_plane), 0)
+        nc.vector.memset(as_i32(r_plane), 0)
+        make_identity(nc, ident[:])
+
+        load_theta(0)
+        load_basis(0)
+        for g in range(2):
+            nc.scalar.dma_start(
+                out=rows[4 * g : 4 * g + 4, :].rearrange("t (q i) -> t q i", i=8),
+                in_=price[512 * g : 512 * g + 512].rearrange("(q t i) -> t q i", t=4, i=8),
+            )
+        load_theta(1)
+        load_basis(1)
+        for src, dst in ((arrive_scales, r_plane), (leave_scales, l_plane)):
+            for q in range(4):
+                nc.sync.dma_start(
+                    out=dst[32 * q : 32 * q + 4].bitcast(I32),
+                    in_=src[:, 4 * q : 4 * q + 4, :].bitcast(I32).rearrange("g r n -> r g n"),
+                )
+        for src, dst in ((arrive_words, r_words), (leave_words, l_words)):
+            nc.sync.dma_start(
+                out=dst[:].bitcast(I32),
+                in_=src.bitcast(I32).rearrange("g p w -> p g w"),
+            )
+        load_basis(2)
+        load_basis(3)
+
+        nc.scalar.activation(out=one[:], in_=one[:], func=ACT.Abs_reciprocal_sqrt)
+
+        th_grp, th_codes, th_sc = [], [], []
+        for h in range(2):
+            a_ = kt("th_grp%d" % h, [P, 512, 4], BF16)
+            b_ = kt("th_codes%d" % h, [P, 512], U32)
+            c_ = kt("th_sc%d" % h, [P, 512], U8)
+            th_grp.append(a_)
+            th_codes.append(b_)
+            th_sc.append(c_)
+
+        def theta_interleave(h, n_scalar):
+            src = th_raw[h][:].rearrange("p j (q t i) -> p t q i j", t=4, i=8)
+            dst = th_grp[h][:].rearrange("p (t q i) j -> p t q i j", t=4, i=8)
+            for t in range(4):
+                if t >= 4 - n_scalar:
+                    nc.scalar.copy(out=dst[:, t], in_=src[:, t])
+                else:
+                    nc.vector.tensor_copy(out=dst[:, t], in_=src[:, t])
+
+        def quant(codes, scales, grp):
+            nc.vector.quantize_mx(
+                out=codes[:].bitcast(FP8X4),
+                scales=scales[:],
+                in_=grp[:].rearrange("p n t -> p (n t)"),
+            )
+
+        ba_grp, ba_codes, ba_sc = {}, [], []
+        for c in range(4):
+            b_ = kt("ba_codes%d" % c, [P, 512], U32)
+            s_ = kt("ba_sc%d" % c, [P, 512], U8)
+            ba_codes.append(b_)
+            ba_sc.append(s_)
+
+        def basis_turn(c, engs):
+            grp = stage.tile([P, 512, 4], BF16, name="ba_grp", tag="ba_grp", align_bytes=64)
+            ba_grp[c] = grp
+            flat = grp[:].rearrange("p a f -> p (a f)").bitcast(F32)
+            for b in range(2):
+                bank = psum.tile([P, 2, 2, P], F32, name="e", tag="e")
+                for rr in range(2):
+                    words = ba_raw[c][:, 2 * b + rr, :].bitcast(F32)
+                    for u in range(2):
+                        nc.tensor.transpose(bank[:, rr, u, :], words[:, u:256:2], ident[:])
+                dst = flat[:, 512 * b : 512 * b + 512].rearrange("p (r a u) -> p r a u", r=2, u=2)
+                src = bank[:].rearrange("p r u a -> p r a u")
+                if engs[b] == "S":
+                    nc.scalar.copy(out=dst, in_=src)
+                else:
+                    nc.vector.tensor_copy(out=dst, in_=src)
+
+        r_tiles = {}
+
+        def c_tile(q, t):
+            c, g = divmod(q, 2)
+            if t == 0:
+                r_ = stage.tile([P, 4, 512], F32, name="r", tag="r", bufs=6, align_bytes=64)
+                r_tiles[q] = r_
+            bank = psum.tile([P, 512], F32, name="c", tag="c")
+            nc.tensor.matmul_mx(
+                out=bank[:],
+                lhsT=th_codes[g][:, P * t : P * t + P].bitcast(FP8X4),
+                lhsT_scale=th_sc[g][:, P * t : P * t + P],
+                rhs=ba_codes[c][:].bitcast(FP8X4),
+                rhs_scale=ba_sc[c][:],
+                start=True,
+                stop=True,
+            )
+            nc.scalar.activation(
+                out=r_tiles[q][:, t, :],
+                in_=bank[:],
+                func=ACT.Abs_reciprocal_sqrt,
+                scale=csc[:, 4 * g + t : 4 * g + t + 1],
+            )
+
+        r2_tiles, m_grp, m_codes, m_sc = {}, {}, {}, {}
+        for q in range(8):
+            b_ = kt("m_codes%d" % q, [P, 512], U32)
+            s_ = kt("m_sc%d" % q, [P, 512], U8)
+            m_codes[q] = b_
+            m_sc[q] = s_
+
+        def square(q, eng):
+            s_ = stage.tile([P, 4, 512], F32, name="r2", tag="r2", align_bytes=64)
+            r2_tiles[q] = s_
+            if eng is nc.gpsimd:
+                for t in range(4):
+                    eng.tensor_tensor(
+                        out=s_[:, t, :], in0=r_tiles[q][:, t, :], in1=r_tiles[q][:, t, :], op=ALU.mult
+                    )
+            else:
+                eng.tensor_tensor(out=s_[:], in0=r_tiles[q][:], in1=r_tiles[q][:], op=ALU.mult)
+
+        def cube(q, lo=0, hi=512):
+            if lo == 0:
+                m_ = stage.tile([P, 512, 4], BF16, name="m_grp", tag="m_grp", align_bytes=64)
+                m_grp[q] = m_
+            nc.vector.tensor_tensor(
+                out=m_grp[q][:, lo:hi, :].rearrange("p (c i) t -> p c t i", i=4),
+                in0=r2_tiles[q][:, :, lo:hi].rearrange("p t (c i) -> p c t i", i=4),
+                in1=r_tiles[q][:, :, lo:hi].rearrange("p t (c i) -> p c t i", i=4),
+                op=ALU.mult,
+            )
+
+        def m_quant(q, lo=0, hi=512):
+            nc.vector.quantize_mx(
+                out=m_codes[q][:, lo:hi].bitcast(FP8X4),
+                scales=m_sc[q][:, lo:hi],
+                in_=m_grp[q][:, lo:hi, :].rearrange("p n t -> p (n t)"),
+            )
+
+        d_grp, d_codes, d_sc = {}, {}, {}
+        for g in range(2):
+            for zh in range(2):
+                b_ = kt("d_codes%d%d" % (g, zh), [P, 512], U32)
+                s_ = kt("d_sc%d%d" % (g, zh), [P, 512], U8)
+                d_codes[g, zh] = b_
+                d_sc[g, zh] = s_
+
+        def permute_arrive():
+            for g in range(2):
+                for h in range(2):
+                    for tile_, perm, w in ((r_words, rp_words, 4), (r_plane, rp_plane, 2)):
+                        n = 64 * w
+                        src = tile_[:, g, :].bitcast(I32)[:, n * h : n * h + n]
+                        dst = perm[:, g, :].bitcast(I32)[:, n * h : n * h + n]
+                        nc.vector.tensor_copy(
+                            out=dst.rearrange("p (t q w) -> p t q w", t=4, w=w),
+                            in_=src.rearrange("p (q t w) -> p t q w", t=4, w=w),
+                        )
+
+        def d_bank(j, eng="V"):
+            zh, rest = divmod(j, 8)
+            gz, zc = divmod(rest, 4)
+            if zc == 0:
+                d_ = stage.tile([P, 512, 4], BF16, name="d_grp", tag="d_grp", align_bytes=64)
+                d_grp[gz, zh] = d_
+            bank = psum.tile([P, 4, P], F32, name="e", tag="e")
+            z0 = 512 * zh + P * zc
+            for t in range(4):
+                n0 = 512 * gz + P * t
+                for g in range(2):
+                    nc.tensor.matmul_mx(
+                        out=bank[:, t, :],
+                        lhsT=rp_words[:, g, 2 * n0 : 2 * n0 + 2 * P].bitcast(FP4X4),
+                        lhsT_scale=rp_plane[:, g, n0 : n0 + P],
+                        rhs=l_words[:, g, 2 * z0 : 2 * z0 + 2 * P].bitcast(FP4X4),
+                        rhs_scale=l_plane[:, g, z0 : z0 + P],
+                        start=(g == 0),
+                        stop=(g == 1),
+                    )
+            dst = d_grp[gz, zh][:, P * zc : P * zc + P, :]
+            src = bank[:].rearrange("p t z -> p z t")
+            if eng == "S":
+                nc.scalar.copy(out=dst, in_=src)
+            else:
+                nc.vector.tensor_copy(out=dst, in_=src)
+
+        def d_quant(j):
+            zh, gz = divmod(j, 2)
+            quant(d_codes[gz, zh], d_sc[gz, zh], d_grp[gz, zh])
+
+        logs = {}
+
+        def e_part(c, rs, zhs=(0, 1)):
+            for zh in zhs:
+                for r in rs:
+                    if (c, r) not in logs:
+                        l_ = stage.tile([P, 1024], F32, name="log", tag="log", bufs=10, align_bytes=64)
+                        logs[c, r] = l_
+                    tag = "e" if r % 2 == 0 else "c"
+                    bank = psum.tile([P, 512], F32, name=tag, tag=tag)
+                    for g in range(2):
+                        nc.tensor.matmul_mx(
+                            out=bank[:],
+                            lhsT=m_codes[2 * c + g][:, P * r : P * r + P].bitcast(FP8X4),
+                            lhsT_scale=m_sc[2 * c + g][:, P * r : P * r + P],
+                            rhs=d_codes[g, zh][:].bitcast(FP8X4),
+                            rhs_scale=d_sc[g, zh][:],
+                            start=(g == 0),
+                            stop=(g == 1),
+                        )
+                    nc.scalar.activation(
+                        out=logs[c, r][:, 512 * zh : 512 * zh + 512], in_=bank[:], func=ACT.Ln
+                    )
+
+        def finish(c):
+            view = out[512 * c : 512 * c + 512, :].rearrange("(p r) z -> r p z", r=4)
+            for r in range(4):
+                l_ = logs[c, r]
+                nc.scalar.activation(out=l_[:], in_=l_[:], func=ACT.Exp, scale=-2.0 / 3.0)
+                nc.sync.dma_start(out=view[r], in_=l_[:])
+
+        theta_interleave(0, 1)
+        nc.vector.tensor_copy(out=rows32[:], in_=rows[:])
+        pbank = psum.tile([P, P], F32, name="e", tag="e")
+        nc.tensor.transpose(pbank[:], rows32[:], ident[:])
+        quant(th_codes[0], th_sc[0], th_grp[0])
+        nc.vector.tensor_copy(out=price_col[:], in_=pbank[:, 0:8])
+        nc.gpsimd.tensor_scalar(
+            out=expo[:], in0=price_col[:], scalar1=0.0, scalar2=-2.0 / 3.0, op0=ALU.mult, op1=ALU.add
+        )
+        nc.gpsimd.tensor_tensor(out=csc[:], in0=price_col[:], in1=expo[:], op=ALU.pow)
+        basis_turn(0, "SV")
+        quant(ba_codes[0], ba_sc[0], ba_grp[0])
+        theta_interleave(1, 0)
+        for t in range(4):
+            c_tile(0, t)
+        quant(th_codes[1], th_sc[1], th_grp[1])
+        basis_turn(1, "VV")
+        permute_arrive()
+        quant(ba_codes[1], ba_sc[1], ba_grp[1])
+        square(0, nc.gpsimd)
+        jd = 0
+        for q in range(1, 8):
+            for t in range(4):
+                c_tile(q, t)
+                if t % 2 == 1 and jd < 16:
+                    d_bank(jd)
+                    jd += 1
+                    if jd in (6, 10, 14):
+                        d_quant(jd // 4 - 1)
+            if q == 2:
+                square(1, nc.gpsimd)
+            if q == 1:
+                basis_turn(2, "VV")
+            if q == 2:
+                quant(ba_codes[2], ba_sc[2], ba_grp[2])
+            if q == 3:
+                basis_turn(3, "VV")
+            if q == 4:
+                quant(ba_codes[3], ba_sc[3], ba_grp[3])
+            if q == 4:
+                cube(0)
+            if q == 5:
+                m_quant(0)
+                cube(1)
+            if q == 6:
+                m_quant(1)
+        d_bank(14)
+        d_bank(15)
+        square(2, nc.vector)
+        d_quant(3)
+        e_part(0, range(4))
+        finish(0)
+        cube(2)
+        square(3, nc.vector)
+        m_quant(2)
+        cube(3)
+        square(4, nc.vector)
+        m_quant(3)
+        e_part(1, range(4))
+        finish(1)
+        cube(4)
+        square(5, nc.vector)
+        m_quant(4)
+        cube(5)
+        square(6, nc.vector)
+        m_quant(5)
+        e_part(2, range(4))
+        square(7, nc.vector)
+        cube(6, 0, 256)
+        cube(7, 0, 256)
+        m_quant(6, 0, 256)
+        m_quant(7, 0, 256)
+        e_part(3, range(2))
+        cube(6, 256, 512)
+        cube(7, 256, 512)
+        m_quant(6, 256, 512)
+        m_quant(7, 256, 512)
+        e_part(3, range(2, 4))
+        finish(2)
+        finish(3)

@@ -17,6 +17,22 @@ ACT = mybir.ActivationFunctionType
 ALU = mybir.AluOpType
 
 P = 128
+LOADS = "th0 ba0 th1 ba1 ba2 sc R L ba3"
+STEPS = (
+    "pc pT th02 th00! pcol th01 pow th03! T00 thq0 T01 bc00 bc01! th12 th13! bq0 T10 th11! th10 C00 "
+    "C01 thq1 A00 C02 T11 bc10 A01 s00 C03 A02 bc11 C10 A03 T20 s01 A10 C11 C12 A11 bq1 C13 T21 A12 "
+    "rp0 C20 A13 rp1 C21 bc20 s02 A20 D0 bc21 A21 C22 C23 s03 A22 C30 D1 A23 C31 bq2 A30 C32 T30 dc1! "
+    "m00 T31 A31 C33 bc30 s10 A32 C40 dc0 A33 D2 s11 A40 C41 dc2 C42 A41 D3 bc31 s12 C43 dc3! D4 A42 "
+    "C50 mq00 D5 A43 bq3 dc4! D6 s13 dc5 A50 C51 C52 dc6! D7 dq0 A51 D8 m10 dc7! D9 A52 dq1 C53 C60 "
+    "dc8! m01 D10 A53 D11 A60 dc9 s20 C61 C62 dc10 A61 D12 mq10 A62 C63 dc11 s21 C70 A63 C71 dc12 D13 "
+    "A70 dq2 C72 A71 C73 dc13 s22 D14 A72 D15 A73 dc14 s23 E000 dc15 L000 dq3 m11 E001 E010 L001 mq01 "
+    "E011 L010 mq11 s30 E020 L011 E021 L020 E030 L021 E031 L030 m20 L031 X00 m30 s40 X01 m21 X02 mq20 "
+    "mq30 X03 m31 E100 E101 L100 m40 E110 E111 mq21 mq31 s50 E120 L101 E121 L110 E130 L111 E131 s60 "
+    "L120 L121 L130 L131 mq40 X10 m50 mq50 m41 E200 E201 X11 m51 E210 E211 X12 mq41 s70 X13 L200 m60 "
+    "mq51 m70 E220 L201 E221 mq60 L210 E230 mq70 L211 m61 E231 L220 E300 m71 L221 E301 L230 E310 mq61 "
+    "L231 E311 mq71 L300 E320 L301 E321 L310 E330 L311 E331 L320 L321 L330 L331 X20 X21 X22 X23 X30 "
+    "X31 X32 X33 "
+)
 
 
 def tile_endogenous_grid_euler_step_s12_kernel(
@@ -26,19 +42,18 @@ def tile_endogenous_grid_euler_step_s12_kernel(
     with ExitStack() as ctx:
         keep = ctx.enter_context(tc.tile_pool(name="keep", bufs=1))
         stage = ctx.enter_context(tc.tile_pool(name="stage", bufs=2))
-        psum = ctx.enter_context(tc.psum_pool(name="psum", bufs=4))
-        ctx.enter_context(
-            tc.manual_schedule(
-                engines={mybir.EngineType.Activation, mybir.EngineType.Pool, mybir.EngineType.SP}
-            )
-        )
+        psum = ctx.enter_context(tc.psum_pool(name="psum", bufs=3))
+        ctx.enter_context(tc.manual_schedule())
 
         def kt(name, shape, dtype):
             return keep.tile(shape, dtype, name=name, tag=name, align_bytes=64)
 
+        def st(tag, shape, dtype, bufs):
+            return stage.tile(shape, dtype, name=tag, tag=tag, bufs=bufs, align_bytes=64)
+
         ident = kt("ident", [P, P], F32)
         one = kt("one", [P, 1], F32)
-        rows = kt("rows", [P, P], BF16)
+        rows = kt("rows", [8, P], BF16)
         rows32 = kt("rows32", [P, P], F32)
         price_col = kt("price_col", [P, 8], F32)
         expo = kt("expo", [P, 8], F32)
@@ -49,181 +64,130 @@ def tile_endogenous_grid_euler_step_s12_kernel(
         l_plane = kt("l_plane", [P, 2, 1024], U8)
         r_plane = kt("r_plane", [P, 2, 1024], U8)
         rp_plane = kt("rp_plane", [P, 2, 1024], U8)
+        th_codes, th_sc, ba_codes, ba_sc, m_codes, m_sc, d_codes, d_sc = {}, {}, {}, {}, {}, {}, {}, {}
+
+        def codes_for(store, scs, label, key):
+            w = kt("%s_codes%s" % (label, key), [P, 512], U32)
+            s = kt("%s_sc%s" % (label, key), [P, 512], U8)
+            store[key] = w
+            scs[key] = s
+
+        for h in range(2):
+            codes_for(th_codes, th_sc, "th", h)
+        for c in range(4):
+            codes_for(ba_codes, ba_sc, "ba", c)
+            codes_for(d_codes, d_sc, "d", c)
+        for q in range(8):
+            codes_for(m_codes, m_sc, "m", q)
 
         def as_i32(t):
             return t[:].rearrange("p g w -> p (g w)").bitcast(I32)
 
-        th_raw = []
-        for h in range(2):
-            t_ = kt("th_raw%d" % h, [P, 4, 512], BF16)
-            th_raw.append(t_)
-        ba_raw = []
-        for c in range(4):
-            b_ = kt("ba_raw%d" % c, [P, 4, 512], BF16)
-            ba_raw.append(b_)
-
-        def load_theta(h):
-            nc.sync.dma_start(
-                out=th_raw[h][:],
-                in_=theta[:, 512 * h : 512 * h + 512].rearrange("(p j) z -> p j z", j=4),
-            )
-
-        def load_basis(c):
-            nc.sync.dma_start(
-                out=ba_raw[c][:],
-                in_=basis[512 * c : 512 * c + 512, :].rearrange("(p r) k -> p r k", r=4),
-            )
-
-        nc.vector.memset(rows[:], 0.0)
         nc.vector.memset(one[:], 1.0)
+        nc.vector.memset(rows32[:], 0.0)
         nc.vector.memset(as_i32(l_plane), 0)
         nc.vector.memset(as_i32(r_plane), 0)
         make_identity(nc, ident[:])
-
-        load_theta(0)
-        load_basis(0)
         for g in range(2):
-            nc.scalar.dma_start(
+            nc.sync.dma_start(
                 out=rows[4 * g : 4 * g + 4, :].rearrange("t (q i) -> t q i", i=8),
                 in_=price[512 * g : 512 * g + 512].rearrange("(q t i) -> t q i", t=4, i=8),
             )
-        load_theta(1)
-        load_basis(1)
-        for src, dst in ((arrive_scales, r_plane), (leave_scales, l_plane)):
-            for q in range(4):
+        th_raw, ba_raw = {}, {}
+        for what in LOADS.split():
+            if what in ("th0", "th1"):
+                h = int(what[2])
+                raw = st("raw", [P, 4, 512], BF16, 12)
+                th_raw[h] = raw
                 nc.sync.dma_start(
-                    out=dst[32 * q : 32 * q + 4].bitcast(I32),
-                    in_=src[:, 4 * q : 4 * q + 4, :].bitcast(I32).rearrange("g r n -> r g n"),
+                    out=raw[:],
+                    in_=theta[:, 512 * h : 512 * h + 512].rearrange("(p j) z -> p j z", j=4),
                 )
-        for src, dst in ((arrive_words, r_words), (leave_words, l_words)):
-            nc.sync.dma_start(
-                out=dst[:].bitcast(I32),
-                in_=src.bitcast(I32).rearrange("g p w -> p g w"),
-            )
-        load_basis(2)
-        load_basis(3)
-
+            elif what == "sc":
+                for src, dst in ((arrive_scales, r_plane), (leave_scales, l_plane)):
+                    for q in range(4):
+                        nc.sync.dma_start(
+                            out=dst[32 * q : 32 * q + 4].bitcast(I32),
+                            in_=src[:, 4 * q : 4 * q + 4, :].bitcast(I32).rearrange("g r n -> r g n"),
+                        )
+            elif what in ("R", "L"):
+                src, dst = (arrive_words, r_words) if what == "R" else (leave_words, l_words)
+                nc.sync.dma_start(
+                    out=dst[:].bitcast(I32), in_=src.bitcast(I32).rearrange("g p w -> p g w")
+                )
+            else:
+                c = int(what[2])
+                raw = st("raw", [P, 4, 512], BF16, 12)
+                ba_raw[c] = raw
+                nc.sync.dma_start(
+                    out=raw[:],
+                    in_=basis[512 * c : 512 * c + 512, :].rearrange("(p r) k -> p r k", r=4),
+                )
         nc.scalar.activation(out=one[:], in_=one[:], func=ACT.Abs_reciprocal_sqrt)
 
-        th_grp, th_codes, th_sc = [], [], []
-        for h in range(2):
-            a_ = kt("th_grp%d" % h, [P, 512, 4], BF16)
-            b_ = kt("th_codes%d" % h, [P, 512], U32)
-            c_ = kt("th_sc%d" % h, [P, 512], U8)
-            th_grp.append(a_)
-            th_codes.append(b_)
-            th_sc.append(c_)
-
-        def theta_interleave(h, n_scalar):
-            src = th_raw[h][:].rearrange("p j (q t i) -> p t q i j", t=4, i=8)
-            dst = th_grp[h][:].rearrange("p (t q i) j -> p t q i j", t=4, i=8)
-            for t in range(4):
-                if t >= 4 - n_scalar:
-                    nc.scalar.copy(out=dst[:, t], in_=src[:, t])
-                else:
-                    nc.vector.tensor_copy(out=dst[:, t], in_=src[:, t])
+        def copy(on_scalar, dst, src):
+            if on_scalar:
+                nc.scalar.copy(out=dst, in_=src)
+            else:
+                nc.vector.tensor_copy(out=dst, in_=src)
 
         def quant(codes, scales, grp):
             nc.vector.quantize_mx(
-                out=codes[:].bitcast(FP8X4),
-                scales=scales[:],
-                in_=grp[:].rearrange("p n t -> p (n t)"),
+                out=codes.bitcast(FP8X4), scales=scales, in_=grp.rearrange("p n t -> p (n t)")
             )
 
-        ba_grp, ba_codes, ba_sc = {}, [], []
-        for c in range(4):
-            b_ = kt("ba_codes%d" % c, [P, 512], U32)
-            s_ = kt("ba_sc%d" % c, [P, 512], U8)
-            ba_codes.append(b_)
-            ba_sc.append(s_)
+        th_grp, ba_grp, d_grp, m_grp, r_t, r2_t, bank, logs = {}, {}, {}, {}, {}, {}, {}, {}
+        cnt = [0]
 
-        def basis_turn(c, engs):
-            grp = stage.tile([P, 512, 4], BF16, name="ba_grp", tag="ba_grp", align_bytes=64)
-            ba_grp[c] = grp
-            flat = grp[:].rearrange("p a f -> p (a f)").bitcast(F32)
-            for b in range(2):
-                bank = psum.tile([P, 2, 2, P], F32, name="e", tag="e")
+        def run(step, on_scalar):
+            if step == "pc":
+                nc.vector.tensor_copy(out=rows32[0:8, :], in_=rows[:])
+            elif step == "pT":
+                b = psum.tile([P, P], F32, name="d", tag="d")
+                bank["p"] = b
+                nc.tensor.transpose(b[:], rows32[:], ident[:])
+            elif step == "pcol":
+                nc.vector.tensor_copy(out=price_col[:], in_=bank["p"][:, 0:8])
+            elif step == "pow":
+                nc.gpsimd.tensor_scalar(
+                    out=expo[:], in0=price_col[:], scalar1=0.0, scalar2=-2.0 / 3.0, op0=ALU.mult, op1=ALU.add
+                )
+                nc.gpsimd.tensor_tensor(out=csc[:], in0=price_col[:], in1=expo[:], op=ALU.pow)
+            elif step[:3] == "thq":
+                h = int(step[3])
+                quant(th_codes[h][:], th_sc[h][:], th_grp[h][:])
+            elif step[:2] == "th":
+                h, t = int(step[2]), int(step[3])
+                if h not in th_grp:
+                    grp = st("raw", [P, 512, 4], BF16, 12)
+                    th_grp[h] = grp
+                src = th_raw[h][:].rearrange("p j (q t i) -> p t q i j", t=4, i=8)
+                dst = th_grp[h][:].rearrange("p (t q i) j -> p t q i j", t=4, i=8)
+                copy(on_scalar, dst[:, t], src[:, t])
+            elif step[0] == "T":
+                c, half = int(step[1]), int(step[2])
+                b = psum.tile([P, 2, 2, P], F32, name="b", tag="b", bufs=2)
+                bank[step] = b
                 for rr in range(2):
-                    words = ba_raw[c][:, 2 * b + rr, :].bitcast(F32)
+                    words = ba_raw[c][:, 2 * half + rr, :].bitcast(F32)
                     for u in range(2):
-                        nc.tensor.transpose(bank[:, rr, u, :], words[:, u:256:2], ident[:])
-                dst = flat[:, 512 * b : 512 * b + 512].rearrange("p (r a u) -> p r a u", r=2, u=2)
-                src = bank[:].rearrange("p r u a -> p r a u")
-                if engs[b] == "S":
-                    nc.scalar.copy(out=dst, in_=src)
-                else:
-                    nc.vector.tensor_copy(out=dst, in_=src)
-
-        r_tiles = {}
-
-        def c_tile(q, t):
-            c, g = divmod(q, 2)
-            if t == 0:
-                r_ = stage.tile([P, 4, 512], F32, name="r", tag="r", bufs=6, align_bytes=64)
-                r_tiles[q] = r_
-            bank = psum.tile([P, 512], F32, name="c", tag="c")
-            nc.tensor.matmul_mx(
-                out=bank[:],
-                lhsT=th_codes[g][:, P * t : P * t + P].bitcast(FP8X4),
-                lhsT_scale=th_sc[g][:, P * t : P * t + P],
-                rhs=ba_codes[c][:].bitcast(FP8X4),
-                rhs_scale=ba_sc[c][:],
-                start=True,
-                stop=True,
-            )
-            nc.scalar.activation(
-                out=r_tiles[q][:, t, :],
-                in_=bank[:],
-                func=ACT.Abs_reciprocal_sqrt,
-                scale=csc[:, 4 * g + t : 4 * g + t + 1],
-            )
-
-        r2_tiles, m_grp, m_codes, m_sc = {}, {}, {}, {}
-        for q in range(8):
-            b_ = kt("m_codes%d" % q, [P, 512], U32)
-            s_ = kt("m_sc%d" % q, [P, 512], U8)
-            m_codes[q] = b_
-            m_sc[q] = s_
-
-        def square(q, eng):
-            s_ = stage.tile([P, 4, 512], F32, name="r2", tag="r2", align_bytes=64)
-            r2_tiles[q] = s_
-            if eng is nc.gpsimd:
-                for t in range(4):
-                    eng.tensor_tensor(
-                        out=s_[:, t, :], in0=r_tiles[q][:, t, :], in1=r_tiles[q][:, t, :], op=ALU.mult
-                    )
-            else:
-                eng.tensor_tensor(out=s_[:], in0=r_tiles[q][:], in1=r_tiles[q][:], op=ALU.mult)
-
-        def cube(q, lo=0, hi=512):
-            if lo == 0:
-                m_ = stage.tile([P, 512, 4], BF16, name="m_grp", tag="m_grp", align_bytes=64)
-                m_grp[q] = m_
-            nc.vector.tensor_tensor(
-                out=m_grp[q][:, lo:hi, :].rearrange("p (c i) t -> p c t i", i=4),
-                in0=r2_tiles[q][:, :, lo:hi].rearrange("p t (c i) -> p c t i", i=4),
-                in1=r_tiles[q][:, :, lo:hi].rearrange("p t (c i) -> p c t i", i=4),
-                op=ALU.mult,
-            )
-
-        def m_quant(q, lo=0, hi=512):
-            nc.vector.quantize_mx(
-                out=m_codes[q][:, lo:hi].bitcast(FP8X4),
-                scales=m_sc[q][:, lo:hi],
-                in_=m_grp[q][:, lo:hi, :].rearrange("p n t -> p (n t)"),
-            )
-
-        d_grp, d_codes, d_sc = {}, {}, {}
-        for g in range(2):
-            for zh in range(2):
-                b_ = kt("d_codes%d%d" % (g, zh), [P, 512], U32)
-                s_ = kt("d_sc%d%d" % (g, zh), [P, 512], U8)
-                d_codes[g, zh] = b_
-                d_sc[g, zh] = s_
-
-        def permute_arrive():
-            for g in range(2):
+                        nc.tensor.transpose(b[:, rr, u, :], words[:, u:256:2], ident[:])
+            elif step[:2] == "bc":
+                c, half = int(step[2]), int(step[3])
+                if c not in ba_grp:
+                    grp = st("ba_grp", [P, 512, 4], BF16, 2)
+                    ba_grp[c] = grp
+                flat = ba_grp[c][:].rearrange("p a f -> p (a f)").bitcast(F32)
+                copy(
+                    on_scalar,
+                    flat[:, 512 * half : 512 * half + 512].rearrange("p (r a u) -> p r a u", r=2, u=2),
+                    bank["T%d%d" % (c, half)][:].rearrange("p r u a -> p r a u"),
+                )
+            elif step[:2] == "bq":
+                c = int(step[2])
+                quant(ba_codes[c][:], ba_sc[c][:], ba_grp[c][:])
+            elif step[:2] == "rp":
+                g = int(step[2])
                 for h in range(2):
                     for tile_, perm, w in ((r_words, rp_words, 4), (r_plane, rp_plane, 2)):
                         n = 64 * w
@@ -233,146 +197,125 @@ def tile_endogenous_grid_euler_step_s12_kernel(
                             out=dst.rearrange("p (t q w) -> p t q w", t=4, w=w),
                             in_=src.rearrange("p (q t w) -> p t q w", t=4, w=w),
                         )
-
-        def d_bank(j, eng="V"):
-            zh, rest = divmod(j, 8)
-            gz, zc = divmod(rest, 4)
-            if zc == 0:
-                d_ = stage.tile([P, 512, 4], BF16, name="d_grp", tag="d_grp", align_bytes=64)
-                d_grp[gz, zh] = d_
-            bank = psum.tile([P, 4, P], F32, name="e", tag="e")
-            z0 = 512 * zh + P * zc
-            for t in range(4):
-                n0 = 512 * gz + P * t
-                for g in range(2):
-                    nc.tensor.matmul_mx(
-                        out=bank[:, t, :],
-                        lhsT=rp_words[:, g, 2 * n0 : 2 * n0 + 2 * P].bitcast(FP4X4),
-                        lhsT_scale=rp_plane[:, g, n0 : n0 + P],
-                        rhs=l_words[:, g, 2 * z0 : 2 * z0 + 2 * P].bitcast(FP4X4),
-                        rhs_scale=l_plane[:, g, z0 : z0 + P],
-                        start=(g == 0),
-                        stop=(g == 1),
-                    )
-            dst = d_grp[gz, zh][:, P * zc : P * zc + P, :]
-            src = bank[:].rearrange("p t z -> p z t")
-            if eng == "S":
-                nc.scalar.copy(out=dst, in_=src)
-            else:
-                nc.vector.tensor_copy(out=dst, in_=src)
-
-        def d_quant(j):
-            zh, gz = divmod(j, 2)
-            quant(d_codes[gz, zh], d_sc[gz, zh], d_grp[gz, zh])
-
-        logs = {}
-
-        def e_part(c, rs, zhs=(0, 1)):
-            for zh in zhs:
-                for r in rs:
-                    if (c, r) not in logs:
-                        l_ = stage.tile([P, 1024], F32, name="log", tag="log", bufs=10, align_bytes=64)
-                        logs[c, r] = l_
-                    tag = "e" if r % 2 == 0 else "c"
-                    bank = psum.tile([P, 512], F32, name=tag, tag=tag)
+            elif step[0] == "C":
+                q, t = int(step[1]), int(step[2])
+                c, g = divmod(q, 2)
+                b = psum.tile([P, 512], F32, name="c", tag="c")
+                bank[step] = b
+                nc.tensor.matmul_mx(
+                    out=b[:],
+                    lhsT=th_codes[g][:, P * t : P * t + P].bitcast(FP8X4),
+                    lhsT_scale=th_sc[g][:, P * t : P * t + P],
+                    rhs=ba_codes[c][:].bitcast(FP8X4),
+                    rhs_scale=ba_sc[c][:],
+                    start=True,
+                    stop=True,
+                )
+            elif step[0] == "A":
+                q, t = int(step[1]), int(step[2])
+                if t == 0:
+                    r_ = st("r", [P, 4, 512], F32, 7)
+                    r_t[q] = r_
+                col = 4 * (q % 2) + t
+                nc.scalar.activation(
+                    out=r_t[q][:, t, :],
+                    in_=bank["C%d%d" % (q, t)][:],
+                    func=ACT.Abs_reciprocal_sqrt,
+                    scale=csc[:, col : col + 1],
+                )
+            elif step[0] == "s":
+                q, t = int(step[1]), int(step[2])
+                if t == 0:
+                    s_ = st("r2", [P, 4, 512], F32, 3)
+                    r2_t[q] = s_
+                if q in (0, 1, 2):
+                    r_ = r_t[q][:, t, :]
+                    nc.gpsimd.tensor_tensor(out=r2_t[q][:, t, :], in0=r_, in1=r_, op=ALU.mult)
+                else:
+                    nc.vector.tensor_tensor(out=r2_t[q][:], in0=r_t[q][:], in1=r_t[q][:], op=ALU.mult)
+            elif step[:2] == "mq":
+                q, lo = int(step[2]), 256 * int(step[3])
+                quant(
+                    m_codes[q][:, lo : lo + 256], m_sc[q][:, lo : lo + 256], m_grp[q][:, lo : lo + 256, :]
+                )
+            elif step[0] == "m":
+                q, lo = int(step[1]), 256 * int(step[2])
+                if lo == 0:
+                    m_ = st("m_grp", [P, 512, 4], BF16, 3)
+                    m_grp[q] = m_
+                nc.vector.tensor_tensor(
+                    out=m_grp[q][:, lo : lo + 256, :].rearrange("p (c i) t -> p c t i", i=4),
+                    in0=r2_t[q][:, :, lo : lo + 256].rearrange("p t (c i) -> p c t i", i=4),
+                    in1=r_t[q][:, :, lo : lo + 256].rearrange("p t (c i) -> p c t i", i=4),
+                    op=ALU.mult,
+                )
+            elif step[0] == "D":
+                j = int(step[1:])
+                zh, rest = divmod(j, 8)
+                gz, zc = divmod(rest, 4)
+                b = psum.tile([P, 4, P], F32, name="d", tag="d")
+                bank[step] = b
+                z0 = 512 * zh + P * zc
+                for t in range(4):
+                    n0 = 512 * gz + P * t
                     for g in range(2):
                         nc.tensor.matmul_mx(
-                            out=bank[:],
-                            lhsT=m_codes[2 * c + g][:, P * r : P * r + P].bitcast(FP8X4),
-                            lhsT_scale=m_sc[2 * c + g][:, P * r : P * r + P],
-                            rhs=d_codes[g, zh][:].bitcast(FP8X4),
-                            rhs_scale=d_sc[g, zh][:],
+                            out=b[:, t, :],
+                            lhsT=rp_words[:, g, 2 * n0 : 2 * n0 + 2 * P].bitcast(FP4X4),
+                            lhsT_scale=rp_plane[:, g, n0 : n0 + P],
+                            rhs=l_words[:, g, 2 * z0 : 2 * z0 + 2 * P].bitcast(FP4X4),
+                            rhs_scale=l_plane[:, g, z0 : z0 + P],
                             start=(g == 0),
                             stop=(g == 1),
                         )
-                    nc.scalar.activation(
-                        out=logs[c, r][:, 512 * zh : 512 * zh + 512], in_=bank[:], func=ACT.Ln
+            elif step[:2] == "dc":
+                j = int(step[2:])
+                k, zc = divmod(j, 4)
+                if k not in d_grp:
+                    d_ = st("d_grp", [P, 512, 4], BF16, 2)
+                    d_grp[k] = d_
+                copy(
+                    on_scalar,
+                    d_grp[k][:, P * zc : P * zc + P, :],
+                    bank["D%d" % j][:].rearrange("p t z -> p z t"),
+                )
+            elif step[:2] == "dq":
+                k = int(step[2])
+                quant(d_codes[k][:], d_sc[k][:], d_grp[k][:])
+            elif step[0] == "E":
+                c, r, zh = int(step[1]), int(step[2]), int(step[3])
+                tag, bufs = (("c", 3), ("d", 3), ("b", 2))[cnt[0] % 8 % 3]
+                cnt[0] += 1
+                b = psum.tile([P, 512], F32, name=tag, tag=tag, bufs=bufs)
+                bank[step] = b
+                for g in range(2):
+                    nc.tensor.matmul_mx(
+                        out=b[:],
+                        lhsT=m_codes[2 * c + g][:, P * r : P * r + P].bitcast(FP8X4),
+                        lhsT_scale=m_sc[2 * c + g][:, P * r : P * r + P],
+                        rhs=d_codes[2 * zh + g][:].bitcast(FP8X4),
+                        rhs_scale=d_sc[2 * zh + g][:],
+                        start=(g == 0),
+                        stop=(g == 1),
                     )
-
-        def finish(c):
-            view = out[512 * c : 512 * c + 512, :].rearrange("(p r) z -> r p z", r=4)
-            for r in range(4):
+            elif step[0] == "L":
+                c, r, zh = int(step[1]), int(step[2]), int(step[3])
+                if (c, r) not in logs:
+                    l_ = st("raw", [P, 1024], F32, 12)
+                    logs[c, r] = l_
+                nc.scalar.activation(
+                    out=logs[c, r][:, 512 * zh : 512 * zh + 512], in_=bank["E" + step[1:]][:], func=ACT.Ln
+                )
+            elif step[0] == "X":
+                c, r = int(step[1]), int(step[2])
                 l_ = logs[c, r]
-                nc.scalar.activation(out=l_[:], in_=l_[:], func=ACT.Exp, scale=-2.0 / 3.0)
-                nc.sync.dma_start(out=view[r], in_=l_[:])
+                view = out[512 * c : 512 * c + 512, :].rearrange("(p r) z -> r p z", r=4)
+                pieces = 2 if (c, r) == (3, 3) else 1
+                w = 1024 // pieces
+                for i in range(pieces):
+                    part = l_[:, w * i : w * i + w]
+                    nc.scalar.activation(out=part, in_=part, func=ACT.Exp, scale=-2.0 / 3.0)
+                    nc.sync.dma_start(out=view[r][:, w * i : w * i + w], in_=part)
 
-        theta_interleave(0, 1)
-        nc.vector.tensor_copy(out=rows32[:], in_=rows[:])
-        pbank = psum.tile([P, P], F32, name="e", tag="e")
-        nc.tensor.transpose(pbank[:], rows32[:], ident[:])
-        quant(th_codes[0], th_sc[0], th_grp[0])
-        nc.vector.tensor_copy(out=price_col[:], in_=pbank[:, 0:8])
-        nc.gpsimd.tensor_scalar(
-            out=expo[:], in0=price_col[:], scalar1=0.0, scalar2=-2.0 / 3.0, op0=ALU.mult, op1=ALU.add
-        )
-        nc.gpsimd.tensor_tensor(out=csc[:], in0=price_col[:], in1=expo[:], op=ALU.pow)
-        basis_turn(0, "SV")
-        quant(ba_codes[0], ba_sc[0], ba_grp[0])
-        theta_interleave(1, 0)
-        for t in range(4):
-            c_tile(0, t)
-        quant(th_codes[1], th_sc[1], th_grp[1])
-        basis_turn(1, "VV")
-        permute_arrive()
-        quant(ba_codes[1], ba_sc[1], ba_grp[1])
-        square(0, nc.gpsimd)
-        jd = 0
-        for q in range(1, 8):
-            for t in range(4):
-                c_tile(q, t)
-                if t % 2 == 1 and jd < 16:
-                    d_bank(jd)
-                    jd += 1
-                    if jd in (6, 10, 14):
-                        d_quant(jd // 4 - 1)
-            if q == 2:
-                square(1, nc.gpsimd)
-            if q == 1:
-                basis_turn(2, "VV")
-            if q == 2:
-                quant(ba_codes[2], ba_sc[2], ba_grp[2])
-            if q == 3:
-                basis_turn(3, "VV")
-            if q == 4:
-                quant(ba_codes[3], ba_sc[3], ba_grp[3])
-            if q == 4:
-                cube(0)
-            if q == 5:
-                m_quant(0)
-                cube(1)
-            if q == 6:
-                m_quant(1)
-        d_bank(14)
-        d_bank(15)
-        square(2, nc.vector)
-        d_quant(3)
-        e_part(0, range(4))
-        finish(0)
-        cube(2)
-        square(3, nc.vector)
-        m_quant(2)
-        cube(3)
-        square(4, nc.vector)
-        m_quant(3)
-        e_part(1, range(4))
-        finish(1)
-        cube(4)
-        square(5, nc.vector)
-        m_quant(4)
-        cube(5)
-        square(6, nc.vector)
-        m_quant(5)
-        e_part(2, range(4))
-        square(7, nc.vector)
-        cube(6, 0, 256)
-        cube(7, 0, 256)
-        m_quant(6, 0, 256)
-        m_quant(7, 0, 256)
-        e_part(3, range(2))
-        cube(6, 256, 512)
-        cube(7, 256, 512)
-        m_quant(6, 256, 512)
-        m_quant(7, 256, 512)
-        e_part(3, range(2, 4))
-        finish(2)
-        finish(3)
+        for step in STEPS.split():
+            run(step.replace("!", ""), "!" in step)

@@ -15,23 +15,25 @@ FP8X4 = mybir.dt.float8_e4m3fn_x4
 FP4X4 = mybir.dt.float4_e2m1fn_x4
 ACT = mybir.ActivationFunctionType
 ALU = mybir.AluOpType
+CUTS = ((0, 256), (256, 512), (256, 384), (384, 512))
 
 P = 128
-LOADS = "th0 ba0 th1 ba1 ba2 sc R L ba3"
+LOADS = "ba0a th0 ba0b pr th1 ba1 ba2 sc R L ba3"
 STEPS = (
-    "pc pT th02 th00! pcol th01 pow th03! T00 thq0 T01 bc00 bc01! th12 th13! bq0 T10 th11! th10 C00 "
-    "C01 thq1 A00 C02 T11 bc10 A01 s00 C03 A02 bc11 C10 A03 T20 s01 A10 C11 C12 A11 bq1 C13 T21 A12 "
-    "rp0 C20 A13 rp1 C21 bc20 s02 A20 D0 bc21 A21 C22 C23 s03 A22 C30 D1 A23 C31 bq2 A30 C32 T30 dc1! "
-    "m00 T31 A31 C33 bc30 s10 A32 C40 dc0 A33 D2 s11 A40 C41 dc2 C42 A41 D3 bc31 s12 C43 dc3! D4 A42 "
-    "C50 mq00 D5 A43 bq3 dc4! D6 s13 dc5 A50 C51 C52 dc6! D7 dq0 A51 D8 m10 dc7! D9 A52 dq1 C53 C60 "
-    "dc8! m01 D10 A53 D11 A60 dc9 s20 C61 C62 dc10 A61 D12 mq10 A62 C63 dc11 s21 C70 A63 C71 dc12 D13 "
-    "A70 dq2 C72 A71 C73 dc13 s22 D14 A72 D15 A73 dc14 s23 E000 dc15 L000 dq3 m11 E001 E010 L001 mq01 "
-    "E011 L010 mq11 s30 E020 L011 E021 L020 E030 L021 E031 L030 m20 L031 X00 m30 s40 X01 m21 X02 mq20 "
-    "mq30 X03 m31 E100 E101 L100 m40 E110 E111 mq21 mq31 s50 E120 L101 E121 L110 E130 L111 E131 s60 "
-    "L120 L121 L130 L131 mq40 X10 m50 mq50 m41 E200 E201 X11 m51 E210 E211 X12 mq41 s70 X13 L200 m60 "
-    "mq51 m70 E220 L201 E221 mq60 L210 E230 mq70 L211 m61 E231 L220 E300 m71 L221 E301 L230 E310 mq61 "
-    "L231 E311 mq71 L300 E320 L301 E321 L310 E330 L311 E331 L320 L321 L330 L331 X20 X21 X22 X23 X30 "
-    "X31 X32 X33 "
+    "T00 bc00! th00 th02! bq00 T01 th01 thq00 th03 bc01! C00a thq01 pc A00a thq02 C01a thq03 A01a "
+    "C02a bq01 C03a pT A02a th13 C00b A03a pcol th11 C01b T10 A00b th10 A01b th12 T11 bc10! s00 C02b "
+    "bc11! C03b thq1 A02b bq1 C10 A03b C11 A10 s01 C12 T20 A11 s02 C13 A12 s03 T21 A13 rp0 C20 rp1 "
+    "bc20! C21 s10 C22 A20 D0 m00 A21 C23 D1 dc0! s11 bc21! D2 s20 A22 C30 bq2 A23 C31 s12 D3 dc1! "
+    "dc2 C32 A30 D4 m01 A31 C33 D5 A32 s13 A33 C40 dc3 C41 A40 C42 s21 D6 A41 s22 C43 A42 dc6 T30 "
+    "A43 s30 T31 dc4! dc5 C50 bc31! D7 dq0 bc30! s23 D8 dc7! mq00 C51 bq3 dc8! D9 m10 A50 C52 D10 "
+    "A51 s31 A52 C53 C60 dc9 A53 C61 dq1 A60 C62 D11 m11 A61 C63 A62 C70 dc11 D12 dc10! mq10 C71 A63 "
+    "dc12 D13 A70 s32 C72 A71 D14 dc13 A72 dq2 C73 D15 A73 dc14 E000 dc15 mq11 dq3 s33 E001 L000 "
+    "mq01 E010 m30 L001 E011 L010 E020 m20 L011 E021 L020 E030 mq30 L021 mq20 E031 m21 L030 E100 "
+    "L031 E101 m31 L100 E110 L101 E111 mq21 L110 mq31 s40 E120 L111 s41 E121 L120 s60 E130 L121 s50 "
+    "E131 L130 s51 L131 s52 s53 s42 s61 X00 s43 m40 X01 m41 X02 m50 X03 s70 X10 mq40 s62 X11 m51 X12 "
+    "s71 s72 X13 s63 mq50 mq51 E200 s73 E201 mq41 m70 E210 E211 L200 m60 E220 L201 E221 L210 E230 "
+    "L211 mq60 mq70 E231 L220 m62 E300 L221 m63 E301 L230 mq62 m72 E310 L231 E311 mq72 L300 m73 E320 "
+    "L301 E321 mq73 mq63 L310 E330 L311 E331 L320 L321 L330 L331 X20 X21 X22 X23 X30 X31 X32 X33 "
 )
 
 
@@ -56,8 +58,6 @@ def tile_endogenous_grid_euler_step_s12_kernel(
         rows = kt("rows", [8, P], BF16)
         rows32 = kt("rows32", [P, P], F32)
         price_col = kt("price_col", [P, 8], F32)
-        expo = kt("expo", [P, 8], F32)
-        csc = kt("csc", [P, 8], F32)
         l_words = kt("l_words", [P, 2, 2048], U8)
         r_words = kt("r_words", [P, 2, 2048], U8)
         rp_words = kt("rp_words", [P, 2, 2048], U8)
@@ -88,14 +88,15 @@ def tile_endogenous_grid_euler_step_s12_kernel(
         nc.vector.memset(as_i32(l_plane), 0)
         nc.vector.memset(as_i32(r_plane), 0)
         make_identity(nc, ident[:])
-        for g in range(2):
-            nc.sync.dma_start(
-                out=rows[4 * g : 4 * g + 4, :].rearrange("t (q i) -> t q i", i=8),
-                in_=price[512 * g : 512 * g + 512].rearrange("(q t i) -> t q i", t=4, i=8),
-            )
         th_raw, ba_raw = {}, {}
         for what in LOADS.split():
-            if what in ("th0", "th1"):
+            if what == "pr":
+                for g in range(2):
+                    nc.sync.dma_start(
+                        out=rows[4 * g : 4 * g + 4, :].rearrange("t (q i) -> t q i", i=8),
+                        in_=price[512 * g : 512 * g + 512].rearrange("(q t i) -> t q i", t=4, i=8),
+                    )
+            elif what in ("th0", "th1"):
                 h = int(what[2])
                 raw = st("raw", [P, 4, 512], BF16, 12)
                 th_raw[h] = raw
@@ -117,12 +118,12 @@ def tile_endogenous_grid_euler_step_s12_kernel(
                 )
             else:
                 c = int(what[2])
-                raw = st("raw", [P, 4, 512], BF16, 12)
-                ba_raw[c] = raw
-                nc.sync.dma_start(
-                    out=raw[:],
-                    in_=basis[512 * c : 512 * c + 512, :].rearrange("(p r) k -> p r k", r=4),
-                )
+                if c not in ba_raw:
+                    raw = st("raw", [P, 4, 512], BF16, 12)
+                    ba_raw[c] = raw
+                view = basis[512 * c : 512 * c + 512, :].rearrange("(p r) k -> p r k", r=4)
+                lo, hi = {"a": (0, 2), "b": (2, 4)}.get(what[3:], (0, 4))
+                nc.sync.dma_start(out=ba_raw[c][:, lo:hi, :], in_=view[:, lo:hi, :])
         nc.scalar.activation(out=one[:], in_=one[:], func=ACT.Abs_reciprocal_sqrt)
 
         def copy(on_scalar, dst, src):
@@ -148,14 +149,10 @@ def tile_endogenous_grid_euler_step_s12_kernel(
                 nc.tensor.transpose(b[:], rows32[:], ident[:])
             elif step == "pcol":
                 nc.vector.tensor_copy(out=price_col[:], in_=bank["p"][:, 0:8])
-            elif step == "pow":
-                nc.gpsimd.tensor_scalar(
-                    out=expo[:], in0=price_col[:], scalar1=0.0, scalar2=-2.0 / 3.0, op0=ALU.mult, op1=ALU.add
-                )
-                nc.gpsimd.tensor_tensor(out=csc[:], in0=price_col[:], in1=expo[:], op=ALU.pow)
             elif step[:3] == "thq":
                 h = int(step[3])
-                quant(th_codes[h][:], th_sc[h][:], th_grp[h][:])
+                lo, hi = (0, 512) if h == 1 else (P * int(step[4]), P * int(step[4]) + P)
+                quant(th_codes[h][:, lo:hi], th_sc[h][:, lo:hi], th_grp[h][:, lo:hi, :])
             elif step[:2] == "th":
                 h, t = int(step[2]), int(step[3])
                 if h not in th_grp:
@@ -185,68 +182,69 @@ def tile_endogenous_grid_euler_step_s12_kernel(
                 )
             elif step[:2] == "bq":
                 c = int(step[2])
-                quant(ba_codes[c][:], ba_sc[c][:], ba_grp[c][:])
+                if c == 0:
+                    lo, hi = 256 * int(step[3]), 256 * int(step[3]) + 256
+                else:
+                    lo, hi = 0, 512
+                quant(ba_codes[c][:, lo:hi], ba_sc[c][:, lo:hi], ba_grp[c][:, lo:hi, :])
             elif step[:2] == "rp":
-                g = int(step[2])
-                for h in range(2):
-                    for tile_, perm, w in ((r_words, rp_words, 4), (r_plane, rp_plane, 2)):
-                        n = 64 * w
-                        src = tile_[:, g, :].bitcast(I32)[:, n * h : n * h + n]
-                        dst = perm[:, g, :].bitcast(I32)[:, n * h : n * h + n]
-                        nc.vector.tensor_copy(
-                            out=dst.rearrange("p (t q w) -> p t q w", t=4, w=w),
-                            in_=src.rearrange("p (q t w) -> p t q w", t=4, w=w),
-                        )
+                src, dst, w = ((r_words, rp_words, 4), (r_plane, rp_plane, 2))[int(step[2])]
+                nc.vector.tensor_copy(
+                    out=as_i32(dst).rearrange("p (h t q w) -> p h t q w", h=4, t=4, w=w),
+                    in_=as_i32(src).rearrange("p (h q t w) -> p h t q w", h=4, t=4, w=w),
+                )
             elif step[0] == "C":
                 q, t = int(step[1]), int(step[2])
                 c, g = divmod(q, 2)
-                b = psum.tile([P, 512], F32, name="c", tag="c")
+                lo, hi = {"a": (0, 256), "b": (256, 512)}.get(step[3:], (0, 512))
+                b = psum.tile([P, hi - lo], F32, name="c", tag="c")
                 bank[step] = b
                 nc.tensor.matmul_mx(
                     out=b[:],
                     lhsT=th_codes[g][:, P * t : P * t + P].bitcast(FP8X4),
                     lhsT_scale=th_sc[g][:, P * t : P * t + P],
-                    rhs=ba_codes[c][:].bitcast(FP8X4),
-                    rhs_scale=ba_sc[c][:],
+                    rhs=ba_codes[c][:, lo:hi].bitcast(FP8X4),
+                    rhs_scale=ba_sc[c][:, lo:hi],
                     start=True,
                     stop=True,
                 )
             elif step[0] == "A":
                 q, t = int(step[1]), int(step[2])
-                if t == 0:
+                lo, hi = {"a": (0, 256), "b": (256, 512)}.get(step[3:], (0, 512))
+                if q not in r_t:
                     r_ = st("r", [P, 4, 512], F32, 7)
                     r_t[q] = r_
-                col = 4 * (q % 2) + t
                 nc.scalar.activation(
-                    out=r_t[q][:, t, :],
-                    in_=bank["C%d%d" % (q, t)][:],
-                    func=ACT.Abs_reciprocal_sqrt,
-                    scale=csc[:, col : col + 1],
+                    out=r_t[q][:, t, lo:hi], in_=bank["C" + step[1:]][:], func=ACT.Abs_reciprocal_sqrt
                 )
             elif step[0] == "s":
                 q, t = int(step[1]), int(step[2])
-                if t == 0:
+                if q not in r2_t:
                     s_ = st("r2", [P, 4, 512], F32, 3)
                     r2_t[q] = s_
-                if q in (0, 1, 2):
-                    r_ = r_t[q][:, t, :]
-                    nc.gpsimd.tensor_tensor(out=r2_t[q][:, t, :], in0=r_, in1=r_, op=ALU.mult)
-                else:
-                    nc.vector.tensor_tensor(out=r2_t[q][:], in0=r_t[q][:], in1=r_t[q][:], op=ALU.mult)
-            elif step[:2] == "mq":
-                q, lo = int(step[2]), 256 * int(step[3])
-                quant(
-                    m_codes[q][:, lo : lo + 256], m_sc[q][:, lo : lo + 256], m_grp[q][:, lo : lo + 256, :]
+                col = 4 * (q % 2) + t
+                nc.vector.scalar_tensor_tensor(
+                    out=r2_t[q][:, t, :],
+                    in0=r_t[q][:, t, :],
+                    scalar=price_col[:, col : col + 1],
+                    in1=r_t[q][:, t, :],
+                    op0=ALU.mult,
+                    op1=ALU.mult,
                 )
+            elif step[:2] == "mq":
+                q = int(step[2])
+                lo, hi = CUTS[int(step[3])]
+                quant(m_codes[q][:, lo:hi], m_sc[q][:, lo:hi], m_grp[q][:, lo:hi, :])
             elif step[0] == "m":
-                q, lo = int(step[1]), 256 * int(step[2])
+                q = int(step[1])
+                lo, hi = CUTS[int(step[2])]
                 if lo == 0:
                     m_ = st("m_grp", [P, 512, 4], BF16, 3)
                     m_grp[q] = m_
                 nc.vector.tensor_tensor(
-                    out=m_grp[q][:, lo : lo + 256, :].rearrange("p (c i) t -> p c t i", i=4),
-                    in0=r2_t[q][:, :, lo : lo + 256].rearrange("p t (c i) -> p c t i", i=4),
-                    in1=r_t[q][:, :, lo : lo + 256].rearrange("p t (c i) -> p c t i", i=4),
+                    out=m_grp[q][:, lo:hi, :].rearrange("p (c i) t -> p c t i", i=4),
+                    in0=r2_t[q][:, :, lo:hi].rearrange("p t (c i) -> p c t i", i=4),
+                    in1=r_t[q][:, :, lo:hi].rearrange("p t (c i) -> p c t i", i=4),
                     op=ALU.mult,
                 )
             elif step[0] == "D":
@@ -310,12 +308,11 @@ def tile_endogenous_grid_euler_step_s12_kernel(
                 c, r = int(step[1]), int(step[2])
                 l_ = logs[c, r]
                 view = out[512 * c : 512 * c + 512, :].rearrange("(p r) z -> r p z", r=4)
-                pieces = 2 if (c, r) == (3, 3) else 1
-                w = 1024 // pieces
-                for i in range(pieces):
-                    part = l_[:, w * i : w * i + w]
+                cuts = (0, 512, 768, 1024) if (c, r) == (3, 3) else (0, 1024)
+                for lo, hi in zip(cuts[:-1], cuts[1:]):
+                    part = l_[:, lo:hi]
                     nc.scalar.activation(out=part, in_=part, func=ACT.Exp, scale=-2.0 / 3.0)
-                    nc.sync.dma_start(out=view[r][:, w * i : w * i + w], in_=part)
+                    nc.sync.dma_start(out=view[r][:, lo:hi], in_=part)
 
         for step in STEPS.split():
             run(step.replace("!", ""), "!" in step)

from contextlib import ExitStack

import concourse.mybir as mybir
from concourse.masks import make_identity

A, K, U, Z = 2048, 512, 1024, 1024
FLOPS = 2 * (A * K * Z + Z * U * Z + A * Z * Z)

F32 = mybir.dt.float32
BF16 = mybir.dt.bfloat16
I32 = mybir.dt.int32
U32 = mybir.dt.uint32
U8 = mybir.dt.uint8
FP8X4 = mybir.dt.float8_e4m3fn_x4
FP4X4 = mybir.dt.float4_e2m1fn_x4
ACT = mybir.ActivationFunctionType
ALU = mybir.AluOpType
CUTS = ((0, 256), (256, 512), (256, 384), (384, 512))

P = 128
LOADS = "ba0a th0 ba0b pr th1 ba1 ba2 sc R L ba3"
STEPS = (
    "T00 bc00! th00 th02! bq00 T01 th01 thq00 th03 bc01! C00a thq01 pc A00a thq02 C01a thq03 A01a "
    "C02a bq01 C03a pT A02a th13 C00b A03a pcol th11 C01b T10 A00b th10 A01b th12 T11 bc10! s00 C02b "
    "bc11! C03b thq1 A02b bq1 C10 A03b C11 A10 s01 C12 T20 A11 s02 C13 A12 s03 T21 A13 rp0 C20 rp1 "
    "bc20! C21 s10 C22 A20 D0 m00 A21 C23 D1 dc0! s11 bc21! D2 s20 A22 C30 bq2 A23 C31 s12 D3 dc1! "
    "dc2 C32 A30 D4 m01 A31 C33 D5 A32 s13 A33 C40 dc3 C41 A40 C42 s21 D6 A41 s22 C43 A42 dc6 T30 "
    "A43 s30 T31 dc4! dc5 C50 bc31! D7 dq0 bc30! s23 D8 dc7! mq00 C51 bq3 dc8! D9 m10 A50 C52 D10 "
    "A51 s31 A52 C53 C60 dc9 A53 C61 dq1 A60 C62 D11 m11 A61 C63 A62 C70 dc11 D12 dc10! mq10 C71 A63 "
    "dc12 D13 A70 s32 C72 A71 D14 dc13 A72 dq2 C73 D15 A73 dc14 E000 dc15 mq11 dq3 s33 E001 L000 "
    "mq01 E010 m30 L001 E011 L010 E020 m20 L011 E021 L020 E030 mq30 L021 mq20 E031 m21 L030 E100 "
    "L031 E101 m31 L100 E110 L101 E111 mq21 L110 mq31 s40 E120 L111 s41 E121 L120 s60 E130 L121 s50 "
    "E131 L130 s51 L131 s52 s53 s42 s61 X00 s43 m40 X01 m41 X02 m50 X03 s70 X10 mq40 s62 X11 m51 X12 "
    "s71 s72 X13 s63 mq50 mq51 E200 s73 E201 mq41 m70 E210 E211 L200 m60 E220 L201 E221 L210 E230 "
    "L211 mq60 mq70 E231 L220 m62 E300 L221 m63 E301 L230 mq62 m72 E310 L231 E311 mq72 L300 m73 E320 "
    "L301 E321 mq73 mq63 L310 E330 L311 E331 L320 L321 L330 L331 X20 X21 X22 X23 X30 X31 X32 X33 "
)


def tile_endogenous_grid_euler_step_s12_kernel(
    tc, basis, theta, price, leave_words, leave_scales, arrive_words, arrive_scales, out
):
    nc = tc.nc
    with ExitStack() as ctx:
        keep = ctx.enter_context(tc.tile_pool(name="keep", bufs=1))
        stage = ctx.enter_context(tc.tile_pool(name="stage", bufs=2))
        psum = ctx.enter_context(tc.psum_pool(name="psum", bufs=3))
        ctx.enter_context(tc.manual_schedule())

        def kt(name, shape, dtype):
            return keep.tile(shape, dtype, name=name, tag=name, align_bytes=64)

        def st(tag, shape, dtype, bufs):
            return stage.tile(shape, dtype, name=tag, tag=tag, bufs=bufs, align_bytes=64)

        ident = kt("ident", [P, P], F32)
        one = kt("one", [P, 1], F32)
        rows = kt("rows", [8, P], BF16)
        rows32 = kt("rows32", [P, P], F32)
        price_col = kt("price_col", [P, 8], F32)
        l_words = kt("l_words", [P, 2, 2048], U8)
        r_words = kt("r_words", [P, 2, 2048], U8)
        rp_words = kt("rp_words", [P, 2, 2048], U8)
        l_plane = kt("l_plane", [P, 2, 1024], U8)
        r_plane = kt("r_plane", [P, 2, 1024], U8)
        rp_plane = kt("rp_plane", [P, 2, 1024], U8)
        th_codes, th_sc, ba_codes, ba_sc, m_codes, m_sc, d_codes, d_sc = {}, {}, {}, {}, {}, {}, {}, {}

        def codes_for(store, scs, label, key):
            w = kt("%s_codes%s" % (label, key), [P, 512], U32)
            s = kt("%s_sc%s" % (label, key), [P, 512], U8)
            store[key] = w
            scs[key] = s

        for h in range(2):
            codes_for(th_codes, th_sc, "th", h)
        for c in range(4):
            codes_for(ba_codes, ba_sc, "ba", c)
            codes_for(d_codes, d_sc, "d", c)
        for q in range(8):
            codes_for(m_codes, m_sc, "m", q)

        def as_i32(t):
            return t[:].rearrange("p g w -> p (g w)").bitcast(I32)

        nc.vector.memset(one[:], 1.0)
        nc.vector.memset(rows32[:], 0.0)
        nc.vector.memset(as_i32(l_plane), 0)
        nc.vector.memset(as_i32(r_plane), 0)
        make_identity(nc, ident[:])
        th_raw, ba_raw = {}, {}
        for what in LOADS.split():
            if what == "pr":
                for g in range(2):
                    nc.sync.dma_start(
                        out=rows[4 * g : 4 * g + 4, :].rearrange("t (q i) -> t q i", i=8),
                        in_=price[512 * g : 512 * g + 512].rearrange("(q t i) -> t q i", t=4, i=8),
                    )
            elif what in ("th0", "th1"):
                h = int(what[2])
                raw = st("raw", [P, 4, 512], BF16, 12)
                th_raw[h] = raw
                nc.sync.dma_start(
                    out=raw[:],
                    in_=theta[:, 512 * h : 512 * h + 512].rearrange("(p j) z -> p j z", j=4),
                )
            elif what == "sc":
                for src, dst in ((arrive_scales, r_plane), (leave_scales, l_plane)):
                    for q in range(4):
                        nc.sync.dma_start(
                            out=dst[32 * q : 32 * q + 4].bitcast(I32),
                            in_=src[:, 4 * q : 4 * q + 4, :].bitcast(I32).rearrange("g r n -> r g n"),
                        )
            elif what in ("R", "L"):
                src, dst = (arrive_words, r_words) if what == "R" else (leave_words, l_words)
                nc.sync.dma_start(
                    out=dst[:].bitcast(I32), in_=src.bitcast(I32).rearrange("g p w -> p g w")
                )
            else:
                c = int(what[2])
                if c not in ba_raw:
                    raw = st("raw", [P, 4, 512], BF16, 12)
                    ba_raw[c] = raw
                view = basis[512 * c : 512 * c + 512, :].rearrange("(p r) k -> p r k", r=4)
                lo, hi = {"a": (0, 2), "b": (2, 4)}.get(what[3:], (0, 4))
                nc.sync.dma_start(out=ba_raw[c][:, lo:hi, :], in_=view[:, lo:hi, :])
        nc.scalar.activation(out=one[:], in_=one[:], func=ACT.Abs_reciprocal_sqrt)

        def copy(on_scalar, dst, src):
            if on_scalar:
                nc.scalar.copy(out=dst, in_=src)
            else:
                nc.vector.tensor_copy(out=dst, in_=src)

        def quant(codes, scales, grp):
            nc.vector.quantize_mx(
                out=codes.bitcast(FP8X4), scales=scales, in_=grp.rearrange("p n t -> p (n t)")
            )

        th_grp, ba_grp, d_grp, m_grp, r_t, r2_t, bank, logs = {}, {}, {}, {}, {}, {}, {}, {}
        cnt = [0]

        def run(step, on_scalar):
            if step == "pc":
                nc.vector.tensor_copy(out=rows32[0:8, :], in_=rows[:])
            elif step == "pT":
                b = psum.tile([P, P], F32, name="d", tag="d")
                bank["p"] = b
                nc.tensor.transpose(b[:], rows32[:], ident[:])
            elif step == "pcol":
                nc.vector.tensor_copy(out=price_col[:], in_=bank["p"][:, 0:8])
            elif step[:3] == "thq":
                h = int(step[3])
                lo, hi = (0, 512) if h == 1 else (P * int(step[4]), P * int(step[4]) + P)
                quant(th_codes[h][:, lo:hi], th_sc[h][:, lo:hi], th_grp[h][:, lo:hi, :])
            elif step[:2] == "th":
                h, t = int(step[2]), int(step[3])
                if h not in th_grp:
                    grp = st("raw", [P, 512, 4], BF16, 12)
                    th_grp[h] = grp
                src = th_raw[h][:].rearrange("p j (q t i) -> p t q i j", t=4, i=8)
                dst = th_grp[h][:].rearrange("p (t q i) j -> p t q i j", t=4, i=8)
                copy(on_scalar, dst[:, t], src[:, t])
            elif step[0] == "T":
                c, half = int(step[1]), int(step[2])
                b = psum.tile([P, 2, 2, P], F32, name="b", tag="b", bufs=2)
                bank[step] = b
                for rr in range(2):
                    words = ba_raw[c][:, 2 * half + rr, :].bitcast(F32)
                    for u in range(2):
                        nc.tensor.transpose(b[:, rr, u, :], words[:, u:256:2], ident[:])
            elif step[:2] == "bc":
                c, half = int(step[2]), int(step[3])
                if c not in ba_grp:
                    grp = st("ba_grp", [P, 512, 4], BF16, 2)
                    ba_grp[c] = grp
                flat = ba_grp[c][:].rearrange("p a f -> p (a f)").bitcast(F32)
                copy(
                    on_scalar,
                    flat[:, 512 * half : 512 * half + 512].rearrange("p (r a u) -> p r a u", r=2, u=2),
                    bank["T%d%d" % (c, half)][:].rearrange("p r u a -> p r a u"),
                )
            elif step[:2] == "bq":
                c = int(step[2])
                if c == 0:
                    lo, hi = 256 * int(step[3]), 256 * int(step[3]) + 256
                else:
                    lo, hi = 0, 512
                quant(ba_codes[c][:, lo:hi], ba_sc[c][:, lo:hi], ba_grp[c][:, lo:hi, :])
            elif step[:2] == "rp":
                src, dst, w = ((r_words, rp_words, 4), (r_plane, rp_plane, 2))[int(step[2])]
                nc.vector.tensor_copy(
                    out=as_i32(dst).rearrange("p (h t q w) -> p h t q w", h=4, t=4, w=w),
                    in_=as_i32(src).rearrange("p (h q t w) -> p h t q w", h=4, t=4, w=w),
                )
            elif step[0] == "C":
                q, t = int(step[1]), int(step[2])
                c, g = divmod(q, 2)
                lo, hi = {"a": (0, 256), "b": (256, 512)}.get(step[3:], (0, 512))
                b = psum.tile([P, hi - lo], F32, name="c", tag="c")
                bank[step] = b
                nc.tensor.matmul_mx(
                    out=b[:],
                    lhsT=th_codes[g][:, P * t : P * t + P].bitcast(FP8X4),
                    lhsT_scale=th_sc[g][:, P * t : P * t + P],
                    rhs=ba_codes[c][:, lo:hi].bitcast(FP8X4),
                    rhs_scale=ba_sc[c][:, lo:hi],
                    start=True,
                    stop=True,
                )
            elif step[0] == "A":
                q, t = int(step[1]), int(step[2])
                lo, hi = {"a": (0, 256), "b": (256, 512)}.get(step[3:], (0, 512))
                if q not in r_t:
                    r_ = st("r", [P, 4, 512], F32, 7)
                    r_t[q] = r_
                nc.scalar.activation(
                    out=r_t[q][:, t, lo:hi], in_=bank["C" + step[1:]][:], func=ACT.Abs_reciprocal_sqrt
                )
            elif step[0] == "s":
                q, t = int(step[1]), int(step[2])
                if q not in r2_t:
                    s_ = st("r2", [P, 4, 512], F32, 3)
                    r2_t[q] = s_
                col = 4 * (q % 2) + t
                nc.vector.scalar_tensor_tensor(
                    out=r2_t[q][:, t, :],
                    in0=r_t[q][:, t, :],
                    scalar=price_col[:, col : col + 1],
                    in1=r_t[q][:, t, :],
                    op0=ALU.mult,
                    op1=ALU.mult,
                )
            elif step[:2] == "mq":
                q = int(step[2])
                lo, hi = CUTS[int(step[3])]
                quant(m_codes[q][:, lo:hi], m_sc[q][:, lo:hi], m_grp[q][:, lo:hi, :])
            elif step[0] == "m":
                q = int(step[1])
                lo, hi = CUTS[int(step[2])]
                if lo == 0:
                    m_ = st("m_grp", [P, 512, 4], BF16, 3)
                    m_grp[q] = m_
                nc.vector.tensor_tensor(
                    out=m_grp[q][:, lo:hi, :].rearrange("p (c i) t -> p c t i", i=4),
                    in0=r2_t[q][:, :, lo:hi].rearrange("p t (c i) -> p c t i", i=4),
                    in1=r_t[q][:, :, lo:hi].rearrange("p t (c i) -> p c t i", i=4),
                    op=ALU.mult,
                )
            elif step[0] == "D":
                j = int(step[1:])
                zh, rest = divmod(j, 8)
                gz, zc = divmod(rest, 4)
                b = psum.tile([P, 4, P], F32, name="d", tag="d")
                bank[step] = b
                z0 = 512 * zh + P * zc
                for t in range(4):
                    n0 = 512 * gz + P * t
                    for g in range(2):
                        nc.tensor.matmul_mx(
                            out=b[:, t, :],
                            lhsT=rp_words[:, g, 2 * n0 : 2 * n0 + 2 * P].bitcast(FP4X4),
                            lhsT_scale=rp_plane[:, g, n0 : n0 + P],
                            rhs=l_words[:, g, 2 * z0 : 2 * z0 + 2 * P].bitcast(FP4X4),
                            rhs_scale=l_plane[:, g, z0 : z0 + P],
                            start=(g == 0),
                            stop=(g == 1),
                        )
            elif step[:2] == "dc":
                j = int(step[2:])
                k, zc = divmod(j, 4)
                if k not in d_grp:
                    d_ = st("d_grp", [P, 512, 4], BF16, 2)
                    d_grp[k] = d_
                copy(
                    on_scalar,
                    d_grp[k][:, P * zc : P * zc + P, :],
                    bank["D%d" % j][:].rearrange("p t z -> p z t"),
                )
            elif step[:2] == "dq":
                k = int(step[2])
                quant(d_codes[k][:], d_sc[k][:], d_grp[k][:])
            elif step[0] == "E":
                c, r, zh = int(step[1]), int(step[2]), int(step[3])
                tag, bufs = (("c", 3), ("d", 3), ("b", 2))[cnt[0] % 8 % 3]
                cnt[0] += 1
                b = psum.tile([P, 512], F32, name=tag, tag=tag, bufs=bufs)
                bank[step] = b
                for g in range(2):
                    nc.tensor.matmul_mx(
                        out=b[:],
                        lhsT=m_codes[2 * c + g][:, P * r : P * r + P].bitcast(FP8X4),
                        lhsT_scale=m_sc[2 * c + g][:, P * r : P * r + P],
                        rhs=d_codes[2 * zh + g][:].bitcast(FP8X4),
                        rhs_scale=d_sc[2 * zh + g][:],
                        start=(g == 0),
                        stop=(g == 1),
                    )
            elif step[0] == "L":
                c, r, zh = int(step[1]), int(step[2]), int(step[3])
                if (c, r) not in logs:
                    l_ = st("raw", [P, 1024], F32, 12)
                    logs[c, r] = l_
                nc.scalar.activation(
                    out=logs[c, r][:, 512 * zh : 512 * zh + 512], in_=bank["E" + step[1:]][:], func=ACT.Ln
                )
            elif step[0] == "X":
                c, r = int(step[1]), int(step[2])
                l_ = logs[c, r]
                view = out[512 * c : 512 * c + 512, :].rearrange("(p r) z -> r p z", r=4)
                cuts = (0, 512, 768, 1024) if (c, r) == (3, 3) else (0, 1024)
                for lo, hi in zip(cuts[:-1], cuts[1:]):
                    part = l_[:, lo:hi]
                    nc.scalar.activation(out=part, in_=part, func=ACT.Exp, scale=-2.0 / 3.0)
                    nc.sync.dma_start(out=view[r][:, lo:hi], in_=part)

        for step in STEPS.split():
            run(step.replace("!", ""), "!" in step)
